import numpy as np
CORES = [24,25,26,27,28,29,30,31,152,153,154,155,156,157,158,159]
N = 16
GROUPS = [[0,1,2,3,4,5,6,7],[8,9,10,11,12,13,14,15]]
def setup_inputs(rng):
    return {"x": rng.standard_normal((N, 128, 256), dtype=np.float32)}
def reference(x):
    y = np.empty((N, 128, 32), x.dtype)
    for g in GROUPS:
        s = x[g].max(axis=0)
        n = len(g); b = x.shape[2] // n
        for i, r in enumerate(g):
            y[r] = s[:, i * b:(i + 1) * b]
    return {"y": y}

@@ -1,0 +1,49 @@
+from concourse.bass import DstId, RemoteDMATransfer
+
+SCRATCH = {
+    "xs": ("sbuf", [128, 256], "float32"),
+    "gath": ("sbuf", [128, 256], "float32"),
+    "res": ("sbuf", [128, 32], "float32"),
+}
+SEMAPHORES = ["loaded", "sent", "arrived", "folded", "stored"]
+
+
+def rank_program(g, core, T, topo):
+    rank = T.rank_of(core)
+    if rank is None:
+        return
+    group = [grp for grp in T.tables["GROUPS"] if rank in grp][0]
+    m = [T.cores[r] for r in group]
+    n = len(m)
+    i = group.index(rank)
+    b = T.x.shape[1] // n
+
+    def dst_id(d):
+        rid, pid = topo.addr(d, core)
+        return DstId(rid=rid, pnc=pid)
+
+    def blk(t, j):
+        return t[:, j * b:(j + 1) * b]
+
+    g.dma_start(T.xs[:], T.x[:]).then_inc(T.sem.loaded, 16)
+    g.wait_ge(T.sem.loaded, 16)
+
+    sends = []
+    for j in range(n):
+        h = j ^ 1
+        if h == i:
+            continue
+        sends.append(RemoteDMATransfer(dst_ids=[dst_id(m[h])], dma_engine_mask=0b11 << (2 * len(sends)),
+                                       remote_sem=T.sem.arrived, src=blk(T.xs, j), dst=blk(T.gath, i)))
+    g.remote_dma_fused(sends, local_sem=T.sem.sent)
+
+    p = i ^ 1
+    g.wait_ge(T.sem.arrived, 2 * (n - 1))
+    srcs = [blk(T.gath, s) for s in range(n) if s != i] + [blk(T.xs, p)]
+    g.remote_dma_fused([RemoteDMATransfer(dst_ids=[dst_id(m[p])], dma_engine_mask=0xFFFF, remote_sem=T.sem.folded,
+                                          srcs=srcs, dsts=[T.res[:]], alu_op=2)], local_sem=T.sem.sent)
+
+    g.wait_ge(T.sem.folded, 16)
+    g.dma_start(T.y[:], T.res[:]).then_inc(T.sem.stored, 16)
+    g.wait_ge(T.sem.stored, 16)
+    g.wait_ge(T.sem.sent, 2 * (n - 1) + 16)

@@ -3,7 +3,7 @@ from concourse.bass import DstId, RemoteDMATransfer
 SCRATCH = {
     "xs": ("sbuf", [128, 256], "float32"),
     "gath": ("sbuf", [128, 256], "float32"),
-    "res": ("sbuf", [128, 32], "float32"),
+    "res": ("dram", [128, 32], "float32"),
 }
 SEMAPHORES = ["loaded", "sent", "arrived", "folded", "stored"]
 

from concourse.bass import DstId, RemoteDMATransfer

SCRATCH = {
    "xs": ("sbuf", [128, 256], "float32"),
    "gath": ("sbuf", [128, 256], "float32"),
    "res": ("dram", [128, 32], "float32"),
}
SEMAPHORES = ["loaded", "sent", "arrived", "folded", "stored"]


def rank_program(g, core, T, topo):
    rank = T.rank_of(core)
    if rank is None:
        return
    group = [grp for grp in T.tables["GROUPS"] if rank in grp][0]
    m = [T.cores[r] for r in group]
    n = len(m)
    i = group.index(rank)
    b = T.x.shape[1] // n

    def dst_id(d):
        rid, pid = topo.addr(d, core)
        return DstId(rid=rid, pnc=pid)

    def blk(t, j):
        return t[:, j * b:(j + 1) * b]

    g.dma_start(T.xs[:], T.x[:]).then_inc(T.sem.loaded, 16)
    g.wait_ge(T.sem.loaded, 16)

    sends = []
    for j in range(n):
        h = j ^ 1
        if h == i:
            continue
        sends.append(RemoteDMATransfer(dst_ids=[dst_id(m[h])], dma_engine_mask=0b11 << (2 * len(sends)),
                                       remote_sem=T.sem.arrived, src=blk(T.xs, j), dst=blk(T.gath, i)))
    g.remote_dma_fused(sends, local_sem=T.sem.sent)

    p = i ^ 1
    g.wait_ge(T.sem.arrived, 2 * (n - 1))
    srcs = [blk(T.gath, s) for s in range(n) if s != i] + [blk(T.xs, p)]
    g.remote_dma_fused([RemoteDMATransfer(dst_ids=[dst_id(m[p])], dma_engine_mask=0xFFFF, remote_sem=T.sem.folded,
                                          srcs=srcs, dsts=[T.res[:]], alu_op=2)], local_sem=T.sem.sent)

    g.wait_ge(T.sem.folded, 16)
    g.dma_start(T.y[:], T.res[:]).then_inc(T.sem.stored, 16)
    g.wait_ge(T.sem.stored, 16)
    g.wait_ge(T.sem.sent, 2 * (n - 1) + 16)
